import numpy as np
import ml_dtypes


def mxq(x, axis, fmt="e4m3"):
    dtype, down = {"e4m3": (ml_dtypes.float8_e4m3fn, 7), "e5m2": (ml_dtypes.float8_e5m2, 14)}[fmt]
    v = np.moveaxis(np.asarray(x, np.float32).astype(ml_dtypes.bfloat16).astype(np.float64), axis, -1)
    blocks = v.reshape(v.shape[:-1] + (-1, 32))
    amax = np.abs(blocks).max(-1, keepdims=True)
    byte = np.maximum(np.where(amax > 0, np.frexp(amax)[1] - 1 + 127, 0) - down, 1)
    scale = np.exp2(byte - 127.0)
    codes = (blocks / scale).astype(np.float32).astype(dtype).astype(np.float64)
    return np.moveaxis((codes * scale).reshape(v.shape), -1, axis)


WIDE = False


def mx_kscale(k):
    if not WIDE:
        return np.ones(k)
    levels = np.array([10, -10, 5, -5, 0])
    if k % 512:
        return np.exp2(np.random.permutation(np.resize(levels, k // 32))).repeat(32)
    a = np.empty((k // 512, 16))
    for p in range(k // 512):
        a[p, :8] = np.random.permutation(np.resize(levels, 8))
        for g in range(8):
            far = levels[np.abs(levels - a[p, g]) >= 10]
            a[p, g + 8] = far[np.random.randint(len(far))]
    return np.exp2(a.ravel()).repeat(32)


def f64(x):
    return np.asarray(x).astype(np.float64)


def striped(idx):
    return np.tile(idx.reshape(-1, 16).T, (8, 1)).astype(np.uint16)


def unstriped(offs):
    return offs[:16].T.reshape(-1).astype(np.int64)


E2M1 = np.array([0.0, 0.5, 1.0, 1.5, 2.0, 3.0, 4.0, 6.0, -0.0, -0.5, -1.0, -1.5, -2.0, -3.0, -4.0, -6.0])


def pack_weight(w, fmt):
    k, n = w.shape
    w = f64(np.asarray(w, np.float32).astype(ml_dtypes.bfloat16)).reshape(k // 32, 32, n)
    amax = np.abs(w).max(1)
    if fmt == "e4m3":
        byte = np.frexp(amax)[1] - 1 + 127 - 7
    else:
        mant, ex = np.frexp(amax / 6.0)
        byte = np.where(mant > 0.5, ex, ex - 1) + 127
    byte = np.clip(np.where(amax > 0, byte, 1), 1, 254)
    scaled = (w * np.exp2(127.0 - byte)[:, None, :]).reshape(k, n).astype(np.float32)
    by_word = np.ascontiguousarray(scaled.reshape(k // 512, 128, 4, n).transpose(0, 1, 3, 2))
    if fmt == "e4m3":
        words = by_word.astype(ml_dtypes.float8_e4m3fn).view(np.uint8)
    else:
        c = by_word.astype(ml_dtypes.float4_e2m1fn).view(np.uint8) & 0xF
        words = (c[..., 0::2] | (c[..., 1::2] << 4)).reshape(k // 512, 128, 2 * n)
    return np.ascontiguousarray(words), np.ascontiguousarray(byte.astype(np.uint8).reshape(k // 512, 16, n))


def unpack_weight(words, scales, fmt):
    g, _, n = scales.shape
    words = np.ascontiguousarray(words).reshape(g, 128, n, -1)
    if fmt == "e4m3":
        vals = words.view(ml_dtypes.float8_e4m3fn).astype(np.float64)
    else:
        nib = np.empty((g, 128, n, 4), np.uint8)
        nib[..., 0::2] = words & 0xF
        nib[..., 1::2] = words >> 4
        vals = E2M1[nib]
    vals = vals * np.repeat(np.exp2(scales.astype(np.float64) - 127.0), 8, axis=1)[..., None]
    return vals.transpose(0, 1, 3, 2).reshape(g * 512, n)


def gelu(v):
    return 0.5 * v * (1.0 + np.tanh(np.sqrt(2.0 / np.pi) * (v + 0.044715 * v**3)))


K, T, E, C, N = 512, 4096, 8, 256, 256
R = 2


def by_expert(wq, xq):
    return np.concatenate([wq[e].T @ xq[:, e * C:(e + 1) * C] for e in range(E)], axis=1)


def setup_inputs():
    n = np.random.standard_normal
    s = mx_kscale(K)[:, None]
    slot_token = np.concatenate([r * (T // R) + np.random.permutation(T // R)[:C // R] for e in range(E) for r in range(R)])
    w = [pack_weight(m, "e2m1") for m in n((E, K, N)) / np.sqrt(K) / s[None]]
    return {
        "xT": (n((K, T)) * s).astype(np.float32),
        "w_words": np.stack([m[0] for m in w]),
        "w_scales": np.stack([m[1] for m in w]),
        "b": (0.3 * n((N, E))).astype(np.float32),
        "offs": striped(slot_token),
    }


def reference(xT, w_words, w_scales, b, offs):
    idx = unstriped(offs)
    w = np.stack([unpack_weight(w_words[e], w_scales[e], "e2m1") for e in range(E)])
    xq = mxq(f64(xT)[:, idx], 0, "e4m3")
    y = by_expert(w, xq)
    y = gelu(y + np.repeat(f64(b), C, axis=1))
    return y.reshape(N, E, R, C // R).transpose(0, 2, 1, 3).reshape(N, E * C)

@@ -1,0 +1,118 @@
+from contextlib import ExitStack
+
+import concourse.mybir as mybir
+
+K, T, E, C, N = 512, 4096, 8, 256, 256
+R = 2
+P = 128
+PACK = 4
+S = E * C
+U = C // R
+FLOPS = 2 * K * N * S
+
+F32 = mybir.dt.float32
+BF16 = mybir.dt.bfloat16
+U32 = mybir.dt.uint32
+I32 = mybir.dt.int32
+U16 = mybir.dt.uint16
+U8 = mybir.dt.uint8
+FP8X4 = mybir.dt.float8_e4m3fn_x4
+FP4X4 = mybir.dt.float4_e2m1fn_x4
+ACT = mybir.ActivationFunctionType
+
+CHUNKS = (1024, 1024, 1024, 512, 256, 256)
+PIECE = 512
+GROUP = 16
+
+
+def tile_moe_eps_lin_gelu_kernel(tc, xT, w_words, w_scales, b, offs, out):
+    nc = tc.nc
+    with ExitStack() as ctx:
+        keep = ctx.enter_context(tc.tile_pool(name="keep", bufs=1))
+        psum = ctx.enter_context(tc.psum_pool(name="psum", bufs=1))
+
+        offsets = keep.tile([P, S // GROUP], U16, name="offsets")
+        codes = keep.tile([P, T], U32, name="codes", align_bytes=256)
+        scales = keep.tile([P, T], U8, name="scales", align_bytes=256)
+        w_sb = keep.tile([P, E, 2 * N], U8, name="w_sb", align_bytes=256)
+        ws_sb = keep.tile([P, E * N], U8, name="ws_sb", align_bytes=256)
+        bias = keep.tile([P, 2, E], F32, name="bias")
+        warm = keep.tile([P, 1], F32, name="warm")
+
+        x_rows = xT.rearrange("(p j) t -> p j t", j=PACK)
+        raws = []
+        t0 = 0
+        for i, w in enumerate(CHUNKS):
+            raw = keep.tile([P, PACK, w], F32, name="raw%d" % i)
+            nc.sync.dma_start(out=raw[:], in_=x_rows[:, :, t0 : t0 + w])
+            raws.append((raw, t0, w))
+            t0 += w
+            if i == 0:
+                nc.sync.dma_start(offsets[:], offs)
+        nc.sync.dma_start(
+            out=w_sb[:].bitcast(I32), in_=w_words.rearrange("e a p c -> p (e a) c").bitcast(I32)
+        )
+        nc.gpsimd.memset(scales[:], 0)
+        nc.vector.memset(warm[:], 0.0)
+        nc.scalar.activation(warm[:], warm[:], ACT.Gelu_apprx_tanh)
+        nc.vector.memset(ws_sb[:].bitcast(I32), 0)
+        for q in range(4):
+            nc.scalar.dma_start(
+                out=ws_sb[32 * q : 32 * q + 4, :].rearrange("q (e n) -> q e n", e=E).bitcast(I32),
+                in_=w_scales[:, 0, 4 * q : 4 * q + 4, :].rearrange("e q n -> q e n").bitcast(I32),
+            )
+        nc.scalar.dma_start(out=bias[:], in_=b.rearrange("(h p) e -> p h e", h=2))
+
+        for i, (raw, t0, w) in enumerate(raws):
+            x4 = keep.tile([P, w, PACK], BF16, name="x4_%d" % i, align_bytes=256)
+            cut = w // 2
+            dst = x4[:].rearrange("p (c i) t -> p c t i", i=4)
+            src = raw[:].rearrange("p t (c i) -> p c t i", i=4)
+            nc.vector.tensor_copy(out=dst[:, : cut // 4], in_=src[:, : cut // 4])
+            nc.scalar.activation(dst[:, cut // 4 :], src[:, cut // 4 :], ACT.Copy)
+            nc.vector.quantize_mx(
+                out=codes[:, t0 : t0 + w].bitcast(FP8X4),
+                scales=scales[:, t0 : t0 + w],
+                in_=x4[:].rearrange("p w j -> p (w j)"),
+            )
+
+        result = keep.tile([P, 2, R, S // R], F32, name="result")
+        out_rows = out.rearrange("(h p) (m c) -> p h m c", h=2, m=R)
+        got_scales = None
+        for g in range(S // PIECE):
+            if g % 2 == 0:
+                got_scales = keep.tile([P, 2 * PIECE], U8, name="got_scales%d" % g, align_bytes=256)
+                lo = g * PIECE // GROUP
+                hi = lo + 2 * PIECE // GROUP
+                nc.vector.tensor_copy(got_scales[:], scales[:].indirect(offsets[:, lo:hi]))
+            got = keep.tile([P, PIECE], U32, name="got%d" % g, align_bytes=256)
+            lo = g * PIECE // GROUP
+            hi = lo + PIECE // GROUP
+            nc.vector.tensor_copy(got[:], codes[:].indirect(offsets[:, lo:hi]))
+            banks = []
+            for k in range(2):
+                e = 2 * g + k
+                bank = psum.tile([P, 2, C], F32, name="bank%d" % e)
+                banks.append(bank)
+                s0 = (g % 2) * PIECE + k * C
+                for h in range(2):
+                    nc.tensor.matmul_mx(
+                        out=bank[:, h, :],
+                        lhsT=w_sb[:, e, 256 * h : 256 * h + 256].bitcast(FP4X4),
+                        lhsT_scale=ws_sb[:, e * N + 128 * h : e * N + 128 * h + 128],
+                        rhs=got[:, k * C : (k + 1) * C].bitcast(FP8X4),
+                        rhs_scale=got_scales[:, s0 : s0 + C],
+                        start=True,
+                        stop=True,
+                    )
+            for h in range(2):
+                for k in range(2):
+                    e = 2 * g + k
+                    nc.scalar.activation(
+                        result[:, h, :, e * U : (e + 1) * U],
+                        banks[k][:, h, :].rearrange("p (m u) -> p m u", m=R),
+                        ACT.Gelu_apprx_tanh,
+                        bias=bias[:, h, e : e + 1],
+                    )
+                c0 = 2 * g * U
+                nc.sync.dma_start(out=out_rows[:, h, :, c0 : c0 + 2 * U], in_=result[:, h, :, c0 : c0 + 2 * U])

@@ -20,7 +20,10 @@ FP8X4 = mybir.dt.float8_e4m3fn_x4
 FP4X4 = mybir.dt.float4_e2m1fn_x4
 ACT = mybir.ActivationFunctionType
 
-CHUNKS = (1024, 1024, 1024, 512, 256, 256)
+LOADS = (
+    ((0, 1024, 640), (1024, 1024, 640), (2048, 1024, 640), (3072, 1024, 640)),
+    ((0, 1024, 0), (1024, 1024, 0), (2048, 1024, 512), (3072, 512, 256), (3584, 512, 320)),
+)
 PIECE = 512
 GROUP = 16
 
@@ -32,8 +35,6 @@ def tile_moe_eps_lin_gelu_kernel(tc, xT, w_words, w_scales, b, offs, out):
         psum = ctx.enter_context(tc.psum_pool(name="psum", bufs=1))
 
         offsets = keep.tile([P, S // GROUP], U16, name="offsets")
-        codes = keep.tile([P, T], U32, name="codes", align_bytes=256)
-        scales = keep.tile([P, T], U8, name="scales", align_bytes=256)
         w_sb = keep.tile([P, E, 2 * N], U8, name="w_sb", align_bytes=256)
         ws_sb = keep.tile([P, E * N], U8, name="ws_sb", align_bytes=256)
         bias = keep.tile([P, 2, E], F32, name="bias")
@@ -41,18 +42,16 @@ def tile_moe_eps_lin_gelu_kernel(tc, xT, w_words, w_scales, b, offs, out):
 
         x_rows = xT.rearrange("(p j) t -> p j t", j=PACK)
         raws = []
-        t0 = 0
-        for i, w in enumerate(CHUNKS):
-            raw = keep.tile([P, PACK, w], F32, name="raw%d" % i)
-            nc.sync.dma_start(out=raw[:], in_=x_rows[:, :, t0 : t0 + w])
-            raws.append((raw, t0, w))
-            t0 += w
-            if i == 0:
-                nc.sync.dma_start(offsets[:], offs)
+        for u in range(2):
+            for t0, w, v in LOADS[u]:
+                raw = keep.tile([P, 2, w], F32, name="raw%d_%d" % (u, t0))
+                nc.sync.dma_start(out=raw[:], in_=x_rows[:, 2 * u : 2 * u + 2, t0 : t0 + w])
+                raws.append(raw)
+                if u == 0 and t0 == 0:
+                    nc.sync.dma_start(offsets[:], offs)
         nc.sync.dma_start(
             out=w_sb[:].bitcast(I32), in_=w_words.rearrange("e a p c -> p (e a) c").bitcast(I32)
         )
-        nc.gpsimd.memset(scales[:], 0)
         nc.vector.memset(warm[:], 0.0)
         nc.scalar.activation(warm[:], warm[:], ACT.Gelu_apprx_tanh)
         nc.vector.memset(ws_sb[:].bitcast(I32), 0)
@@ -63,45 +62,57 @@ def tile_moe_eps_lin_gelu_kernel(tc, xT, w_words, w_scales, b, offs, out):
             )
         nc.scalar.dma_start(out=bias[:], in_=b.rearrange("(h p) e -> p h e", h=2))
 
-        for i, (raw, t0, w) in enumerate(raws):
-            x4 = keep.tile([P, w, PACK], BF16, name="x4_%d" % i, align_bytes=256)
-            cut = w // 2
-            dst = x4[:].rearrange("p (c i) t -> p c t i", i=4)
-            src = raw[:].rearrange("p t (c i) -> p c t i", i=4)
-            nc.vector.tensor_copy(out=dst[:, : cut // 4], in_=src[:, : cut // 4])
-            nc.scalar.activation(dst[:, cut // 4 :], src[:, cut // 4 :], ACT.Copy)
-            nc.vector.quantize_mx(
-                out=codes[:, t0 : t0 + w].bitcast(FP8X4),
-                scales=scales[:, t0 : t0 + w],
-                in_=x4[:].rearrange("p w j -> p (w j)"),
-            )
+        tables = []
+        pieces = []
+        for u in range(2):
+            table = keep.tile([P, T, 2], BF16, name="table%d" % u, align_bytes=256)
+            tables.append(table)
+            for i, (t0, w, v) in enumerate(LOADS[u]):
+                raw = raws[len(LOADS[0]) * u + i]
+                dst = table[:, t0 : t0 + w, :].rearrange("p (c i) j -> p c j i", i=4)
+                src = raw[:].rearrange("p j (c i) -> p c j i", i=4)
+                if v > 0:
+                    nc.vector.tensor_copy(out=dst[:, : v // 4], in_=src[:, : v // 4])
+                if v < w:
+                    nc.scalar.activation(dst[:, v // 4 :], src[:, v // 4 :], ACT.Copy)
+            if u == 0:
+                words = table[:].rearrange("p t j -> p (t j)").bitcast(U32)
+                for g in range(S // PIECE):
+                    x4 = keep.tile([P, PIECE, PACK], BF16, name="x4_%d" % g, align_bytes=256)
+                    pieces.append(x4)
+                    lo = g * PIECE // GROUP
+                    hi = lo + PIECE // GROUP
+                    dst = x4[:].rearrange("p n j -> p (n j)").bitcast(U32).rearrange("p (n u) -> p n u", u=2)
+                    nc.vector.tensor_copy(dst[:, :, 0], words.indirect(offsets[:, lo:hi]))
 
         result = keep.tile([P, 2, R, S // R], F32, name="result")
         out_rows = out.rearrange("(h p) (m c) -> p h m c", h=2, m=R)
-        got_scales = None
-        for g in range(S // PIECE):
-            if g % 2 == 0:
-                got_scales = keep.tile([P, 2 * PIECE], U8, name="got_scales%d" % g, align_bytes=256)
-                lo = g * PIECE // GROUP
-                hi = lo + 2 * PIECE // GROUP
-                nc.vector.tensor_copy(got_scales[:], scales[:].indirect(offsets[:, lo:hi]))
-            got = keep.tile([P, PIECE], U32, name="got%d" % g, align_bytes=256)
+        words = tables[1][:].rearrange("p t j -> p (t j)").bitcast(U32)
+
+        def gather(g):
             lo = g * PIECE // GROUP
             hi = lo + PIECE // GROUP
-            nc.vector.tensor_copy(got[:], codes[:].indirect(offsets[:, lo:hi]))
+            dst = pieces[g][:].rearrange("p n j -> p (n j)").bitcast(U32).rearrange("p (n u) -> p n u", u=2)
+            nc.vector.tensor_copy(dst[:, :, 1], words.indirect(offsets[:, lo:hi]))
+
+        def finish(g):
+            codes = keep.tile([P, PIECE], U32, name="codes%d" % g, align_bytes=256)
+            scales = keep.tile([P, PIECE], U8, name="scales%d" % g, align_bytes=256)
+            nc.vector.quantize_mx(
+                out=codes[:].bitcast(FP8X4), scales=scales[:], in_=pieces[g][:].rearrange("p n j -> p (n j)")
+            )
             banks = []
             for k in range(2):
                 e = 2 * g + k
                 bank = psum.tile([P, 2, C], F32, name="bank%d" % e)
                 banks.append(bank)
-                s0 = (g % 2) * PIECE + k * C
                 for h in range(2):
                     nc.tensor.matmul_mx(
                         out=bank[:, h, :],
                         lhsT=w_sb[:, e, 256 * h : 256 * h + 256].bitcast(FP4X4),
                         lhsT_scale=ws_sb[:, e * N + 128 * h : e * N + 128 * h + 128],
-                        rhs=got[:, k * C : (k + 1) * C].bitcast(FP8X4),
-                        rhs_scale=got_scales[:, s0 : s0 + C],
+                        rhs=codes[:, k * C : (k + 1) * C].bitcast(FP8X4),
+                        rhs_scale=scales[:, k * C : (k + 1) * C],
                         start=True,
                         stop=True,
                     )
@@ -116,3 +127,9 @@ def tile_moe_eps_lin_gelu_kernel(tc, xT, w_words, w_scales, b, offs, out):
                     )
                 c0 = 2 * g * U
                 nc.sync.dma_start(out=out_rows[:, h, :, c0 : c0 + 2 * U], in_=result[:, h, :, c0 : c0 + 2 * U])
+
+        for g in range(S // PIECE):
+            gather(g)
+            if g > 0:
+                finish(g - 1)
+        finish(S // PIECE - 1)

from contextlib import ExitStack

import concourse.mybir as mybir

K, T, E, C, N = 512, 4096, 8, 256, 256
R = 2
P = 128
PACK = 4
S = E * C
U = C // R
FLOPS = 2 * K * N * S

F32 = mybir.dt.float32
BF16 = mybir.dt.bfloat16
U32 = mybir.dt.uint32
I32 = mybir.dt.int32
U16 = mybir.dt.uint16
U8 = mybir.dt.uint8
FP8X4 = mybir.dt.float8_e4m3fn_x4
FP4X4 = mybir.dt.float4_e2m1fn_x4
ACT = mybir.ActivationFunctionType

LOADS = (
    ((0, 1024, 640), (1024, 1024, 640), (2048, 1024, 640), (3072, 1024, 640)),
    ((0, 1024, 0), (1024, 1024, 0), (2048, 1024, 512), (3072, 512, 256), (3584, 512, 320)),
)
PIECE = 512
GROUP = 16


def tile_moe_eps_lin_gelu_kernel(tc, xT, w_words, w_scales, b, offs, out):
    nc = tc.nc
    with ExitStack() as ctx:
        keep = ctx.enter_context(tc.tile_pool(name="keep", bufs=1))
        psum = ctx.enter_context(tc.psum_pool(name="psum", bufs=1))

        offsets = keep.tile([P, S // GROUP], U16, name="offsets")
        w_sb = keep.tile([P, E, 2 * N], U8, name="w_sb", align_bytes=256)
        ws_sb = keep.tile([P, E * N], U8, name="ws_sb", align_bytes=256)
        bias = keep.tile([P, 2, E], F32, name="bias")
        warm = keep.tile([P, 1], F32, name="warm")

        x_rows = xT.rearrange("(p j) t -> p j t", j=PACK)
        raws = []
        for u in range(2):
            for t0, w, v in LOADS[u]:
                raw = keep.tile([P, 2, w], F32, name="raw%d_%d" % (u, t0))
                nc.sync.dma_start(out=raw[:], in_=x_rows[:, 2 * u : 2 * u + 2, t0 : t0 + w])
                raws.append(raw)
                if u == 0 and t0 == 0:
                    nc.sync.dma_start(offsets[:], offs)
        nc.sync.dma_start(
            out=w_sb[:].bitcast(I32), in_=w_words.rearrange("e a p c -> p (e a) c").bitcast(I32)
        )
        nc.vector.memset(warm[:], 0.0)
        nc.scalar.activation(warm[:], warm[:], ACT.Gelu_apprx_tanh)
        nc.vector.memset(ws_sb[:].bitcast(I32), 0)
        for q in range(4):
            nc.scalar.dma_start(
                out=ws_sb[32 * q : 32 * q + 4, :].rearrange("q (e n) -> q e n", e=E).bitcast(I32),
                in_=w_scales[:, 0, 4 * q : 4 * q + 4, :].rearrange("e q n -> q e n").bitcast(I32),
            )
        nc.scalar.dma_start(out=bias[:], in_=b.rearrange("(h p) e -> p h e", h=2))

        tables = []
        pieces = []
        for u in range(2):
            table = keep.tile([P, T, 2], BF16, name="table%d" % u, align_bytes=256)
            tables.append(table)
            for i, (t0, w, v) in enumerate(LOADS[u]):
                raw = raws[len(LOADS[0]) * u + i]
                dst = table[:, t0 : t0 + w, :].rearrange("p (c i) j -> p c j i", i=4)
                src = raw[:].rearrange("p j (c i) -> p c j i", i=4)
                if v > 0:
                    nc.vector.tensor_copy(out=dst[:, : v // 4], in_=src[:, : v // 4])
                if v < w:
                    nc.scalar.activation(dst[:, v // 4 :], src[:, v // 4 :], ACT.Copy)
            if u == 0:
                words = table[:].rearrange("p t j -> p (t j)").bitcast(U32)
                for g in range(S // PIECE):
                    x4 = keep.tile([P, PIECE, PACK], BF16, name="x4_%d" % g, align_bytes=256)
                    pieces.append(x4)
                    lo = g * PIECE // GROUP
                    hi = lo + PIECE // GROUP
                    dst = x4[:].rearrange("p n j -> p (n j)").bitcast(U32).rearrange("p (n u) -> p n u", u=2)
                    nc.vector.tensor_copy(dst[:, :, 0], words.indirect(offsets[:, lo:hi]))

        result = keep.tile([P, 2, R, S // R], F32, name="result")
        out_rows = out.rearrange("(h p) (m c) -> p h m c", h=2, m=R)
        words = tables[1][:].rearrange("p t j -> p (t j)").bitcast(U32)

        def gather(g):
            lo = g * PIECE // GROUP
            hi = lo + PIECE // GROUP
            dst = pieces[g][:].rearrange("p n j -> p (n j)").bitcast(U32).rearrange("p (n u) -> p n u", u=2)
            nc.vector.tensor_copy(dst[:, :, 1], words.indirect(offsets[:, lo:hi]))

        def finish(g):
            codes = keep.tile([P, PIECE], U32, name="codes%d" % g, align_bytes=256)
            scales = keep.tile([P, PIECE], U8, name="scales%d" % g, align_bytes=256)
            nc.vector.quantize_mx(
                out=codes[:].bitcast(FP8X4), scales=scales[:], in_=pieces[g][:].rearrange("p n j -> p (n j)")
            )
            banks = []
            for k in range(2):
                e = 2 * g + k
                bank = psum.tile([P, 2, C], F32, name="bank%d" % e)
                banks.append(bank)
                for h in range(2):
                    nc.tensor.matmul_mx(
                        out=bank[:, h, :],
                        lhsT=w_sb[:, e, 256 * h : 256 * h + 256].bitcast(FP4X4),
                        lhsT_scale=ws_sb[:, e * N + 128 * h : e * N + 128 * h + 128],
                        rhs=codes[:, k * C : (k + 1) * C].bitcast(FP8X4),
                        rhs_scale=scales[:, k * C : (k + 1) * C],
                        start=True,
                        stop=True,
                    )
            for h in range(2):
                for k in range(2):
                    e = 2 * g + k
                    nc.scalar.activation(
                        result[:, h, :, e * U : (e + 1) * U],
                        banks[k][:, h, :].rearrange("p (m u) -> p m u", m=R),
                        ACT.Gelu_apprx_tanh,
                        bias=bias[:, h, e : e + 1],
                    )
                c0 = 2 * g * U
                nc.sync.dma_start(out=out_rows[:, h, :, c0 : c0 + 2 * U], in_=result[:, h, :, c0 : c0 + 2 * U])

        for g in range(S // PIECE):
            gather(g)
            if g > 0:
                finish(g - 1)
        finish(S // PIECE - 1)
